import numpy as np, ml_dtypes
CORES = [24,25,26,27,28,29,30,31]
N = 8
import mx_ref
BF = ml_dtypes.bfloat16
def f(rng, *shape):
    return mx_ref.flush((rng.standard_normal(shape, dtype=np.float32) * np.exp2(rng.integers(-2, 3, shape[:-1] + (1,)))).astype(BF))
def wide(rng, *shape, cols=0):
    v = rng.standard_normal(shape, dtype=np.float32) * np.exp2(rng.integers(-12, 13, shape)).astype(np.float32)
    if cols: v *= np.repeat(np.exp2(rng.integers(-cols, cols + 1, shape[:-2] + (1, shape[-1] // 4))) * (rng.random(shape[:-2] + (1, shape[-1] // 4)) > 0.0625), 4, axis=-1).astype(np.float32)
    return mx_ref.flush(v.astype(BF))
T, NB, CH, BW = 512, 4, 64, 128
def scores(x, u):
    return np.stack([mx_ref.matmul(mx_ref.quantize(u[s]), mx_ref.quantize(x[s]))[0] for s in range(N)]) + np.float32(0.0)
def dealt(rng, d, place):
    v = d["x"].reshape(N, 128, T, 4).transpose(0, 2, 1, 3).reshape(N * T, 128, 4)
    g = np.argsort(-scores(d["x"], d["u"]).reshape(-1), kind="stable")
    e = np.stack([g[rng.permutation(place[s])] for s in range(N)])
    return np.ascontiguousarray(v[e].transpose(0, 2, 1, 3)).reshape(N, 128, 4 * T)
def setup_inputs(rng):
    u = np.zeros((N, 128, 512), BF); u[:, :, :4] = f(rng, 128, 4)
    return {"x": f(rng, N, 128, 4 * T), "u": u, "w": f(rng, N, 128, 512 * NB)}
def setup_inputs_ties(rng):
    d = setup_inputs(rng); d["u"][:, 64:] = 0; few = f(rng, 64, 24).reshape(64, 6, 4)
    for s in range(N):
        e = rng.permutation(np.concatenate([np.arange(6), rng.choice(6, T - 6, p=rng.dirichlet(np.ones(6)))]))
        d["x"][s, :64] = few[:, e].reshape(64, -1)
    return d
def setup_inputs_blocks(rng):
    d = setup_inputs(rng); d["x"] = dealt(rng, d, np.arange(N * T).reshape(N, T)[rng.permutation(N)]); return d
def setup_inputs_alternate(rng):
    d = setup_inputs(rng); d["x"] = dealt(rng, d, np.arange(N * T).reshape(T, N).T[rng.permutation(N)]); return d
def setup_inputs_zeros(rng):
    d = setup_inputs(rng); d["u"][:, 64:] = 0
    for s in rng.permutation(N)[:N // 2]: d["x"][s, :64] = 0
    return d
def setup_inputs_spread(rng):
    d = setup_inputs(rng); k = np.where(rng.permutation(N) < N // 2, np.float32(2.0 ** -20), np.float32(2.0 ** 7))
    d["x"] = mx_ref.flush((wide(rng, N, 128, 4 * T, cols=8).astype(np.float32) * k[:, None, None]).astype(BF))
    d["u"] = (d["u"].astype(np.float32) * np.float32(2 ** 24)).astype(BF); return d
def check_inputs(d):
    b = []; u = np.asarray(d["u"]).astype(np.float32)
    for r in range(N):
        if (u[r][:, 4:] != 0).any() or (u[r] != u[0]).any(): b.append("u")
    return b
def reference(x, u, w):
    score = scores(x, u)
    order = [np.argsort(-score[s], kind="stable") for s in range(N)]
    y = np.zeros((N, 128, T), np.float32); ids = np.zeros((N, 2, T), np.float32)
    for d in range(N):
        runs = [order[s][CH * d:CH * d + CH] for s in range(N)]
        rank = np.repeat(np.arange(N), CH); col = np.concatenate(runs)
        m = np.argsort(-score[rank, col], kind="stable")
        rank, col = rank[m], col[m]
        ids[d, 0], ids[d, 1] = rank, col
        t = np.ascontiguousarray(x.reshape(N, 128, T, 4)[rank, :, col].transpose(1, 0, 2)).reshape(128, 4 * T)
        for k in range(NB):
            W = mx_ref.quantize(np.ascontiguousarray(w[d][:, 512 * k:512 * k + 512]))
            y[d][:, BW * k:BW * k + BW] = mx_ref.matmul(W, mx_ref.quantize(np.ascontiguousarray(t[:, 4 * BW * k:4 * BW * k + 4 * BW])))
    return {"y": y, "ids": ids}

@@ -1,0 +1,372 @@
+from concourse.bass import DstId, RemoteDMATransfer
+from concourse.mybir import dt, AluOpType, ActivationFunctionType
+
+F32, BF, I32, U16 = "float32", "bfloat16", "int32", "uint16"
+CODE, PLANE = "float8_e4m3fn_x4", "uint8"
+SCRATCH = {
+    "usm": ("sbuf", [128, 4], BF), "ut": ("sbuf", [128, 512], BF),
+    "xt": ("sbuf", [128, 2048], BF), "wt": ("sbuf", [128, 2048], BF),
+    "uq": ("sbuf", [128, 128], CODE), "up": ("sbuf", [128, 128], PLANE),
+    "urq": ("sbuf", [128, 128], CODE), "urp": ("sbuf", [128, 128], PLANE),
+    "xq": ("sbuf", [128, 512], CODE), "xp": ("sbuf", [128, 512], PLANE),
+    "wq": ("sbuf", [128, 512], CODE), "wp": ("sbuf", [128, 512], PLANE),
+    "slotq": ("sbuf", [128, 512], CODE), "slotp": ("sbuf", [128, 512], PLANE),
+    "landq": ("sbuf", [128, 512], CODE), "landp": ("sbuf", [128, 512], PLANE),
+    "finq": ("sbuf", [128, 512], CODE), "finp": ("sbuf", [128, 512], PLANE),
+    "zoff": ("sbuf", [128, 8], U16), "mk1": ("sbuf", [128, 128], F32), "mk": ("sbuf", [128, 128], F32),
+    "pi": ("sbuf", [128, 1], I32), "pa": ("sbuf", [128, 1], I32), "pb": ("sbuf", [128, 1], I32),
+    "pc": ("sbuf", [128, 1], I32), "g16": ("sbuf", [128, 1], F32), "hi": ("sbuf", [128, 1], F32),
+    "lo": ("sbuf", [128, 1], F32), "run0": ("sbuf", [128, 1], F32), "vfree": ("sbuf", [128, 64], F32),
+    "vals": ("sbuf", [128, 64], BF),
+    "ss0": ("sbuf", [128, 32], F32), "tt1": ("sbuf", [128, 128], F32), "tt2": ("sbuf", [128, 128], F32),
+    "pp": ("sbuf", [128, 4], F32), "dl": ("sbuf", [128, 4], F32), "thr": ("sbuf", [128, 512], F32),
+    "cmp": ("sbuf", [128, 2048], BF), "so": ("sbuf", [128, 1024], BF),
+    "ut1": ("sbuf", [128, 128], F32), "ut2": ("sbuf", [128, 256], F32), "qp": ("sbuf", [128, 4], F32),
+    "cmq": ("sbuf", [128, 1792], BF), "sq": ("sbuf", [128, 896], BF),
+    "colf": ("sbuf", [32, 16], F32), "ocol": ("dram", [128, 4], F32), "rcol": ("dram", [8, 128, 4], F32),
+    "cr": ("sbuf", [128, 512], F32), "idb": ("sbuf", [128, 512], F32), "yb": ("sbuf", [128, 512], F32),
+}
+for _k in "ab":
+    SCRATCH["pl" + _k] = ("sbuf", [128, 4], U16)
+    SCRATCH["sw" + _k] = ("sbuf", [128, 512], BF)
+    SCRATCH["tr" + _k] = ("sbuf", [128, 512], BF)
+    SCRATCH["ya" + _k] = ("sbuf", [128, 16], BF)
+    SCRATCH["g1" + _k] = ("sbuf", [128, 16], BF)
+    SCRATCH["g2" + _k] = ("sbuf", [128, 16], BF)
+    SCRATCH["g3" + _k] = ("sbuf", [128, 16], BF)
+    SCRATCH["xm" + _k] = ("sbuf", [128, 32], BF)
+    SCRATCH["xx" + _k] = ("sbuf", [128, 32], BF)
+    SCRATCH["fo" + _k] = ("sbuf", [128, 32], BF)
+    SCRATCH["zz" + _k] = ("sbuf", [128, 32], BF)
+    SCRATCH["off" + _k] = ("sbuf", [128, 32], U16)
+for _k in range(8):
+    SCRATCH["ps%d" % _k] = ("psum", [128, 512], F32)
+
+SEMAPHORES = ["cv", "cs", "ct", "cg", "du", "dx0", "dx1", "dx2", "dx3", "dw", "dc", "dr", "dy", "di",
+              "ara", "arb", "arc", "ls"]
+
+
+def rank_program(g, core, T, topo):
+    me = T.rank_of(core)
+    if me is None:
+        return
+    V, S, P, Y = g.vector, g.scalar, g.tensor, g.sync
+    Copy, Ident, Abs = ActivationFunctionType.Copy, ActivationFunctionType.Identity, ActivationFunctionType.Abs
+    GT, GE, ADD, MUL = AluOpType.is_gt, AluOpType.is_ge, AluOpType.add, AluOpType.mult
+    AND = AluOpType.bitwise_and
+    cnt, seen = {}, {}
+    queue = {"v": V, "s": S, "t": P, "g": g, "y": Y}
+    CORES = T.cores
+    N = len(CORES)
+    CH = 512 // N
+
+    def need(q, *toks):
+        for sem, val in toks:
+            if seen.get((q, sem), 0) < val:
+                queue[q].wait_ge(T.sem[sem], val)
+                seen[(q, sem)] = val
+
+    def done(q, inst):
+        sem = "c" + q
+        inst.then_inc(T.sem[sem], 1)
+        cnt[sem] = cnt.get(sem, 0) + 1
+        return (sem, cnt[sem])
+
+    def dma(sem, inst):
+        inst.then_inc(T.sem[sem], 16)
+        cnt[sem] = cnt.get(sem, 0) + 16
+        return (sem, cnt[sem])
+
+    tu = dma("du", S.dma_start(T.usm[:], T.u[:, 0:4]))
+    tx = [None] * 4
+    for c in range(4):
+        tx[c] = dma("dx%d" % c, (Y, S)[c % 2].dma_start(T.xt[:, 512 * c:512 * c + 512], T.x[:, 512 * c:512 * c + 512]))
+    need("y", *tx)
+    dma("dw", Y.dma_start(T.wt[:, 0:1024], T.w[:, 0:1024]))
+    tw = dma("dw", Y.dma_start(T.wt[:, 1024:2048], T.w[:, 1024:2048]))
+
+    tpi = done("g", g.iota(T.pi[:], [[1, 1]], 0, 1))
+    tvf = done("g", g.iota(T.vfree[:], [[128, 4], [1, 16]], -256, 0, allow_small_or_imprecise_dtypes=True))
+    tut = done("v", V.memset(T.ut[:], 0.0))
+    tzo = done("v", V.memset(T.zoff[:], 0))
+    tm1 = done("v", V.memset(T.mk1[:], -1.0))
+    tsw = {"a": done("v", V.memset(T.swa[:], 0.0)), "b": done("v", V.memset(T.swb[:], 0.0))}
+    need("g", tm1)
+    tmk = done("g", g.affine_select(T.mk[:], T.mk1[:], [[-1, 128]], GT, 0.0, 0, 1))
+    tcr = done("g", g.iota(T.cr[:], [[1, N], [0, CH]], 0, 0, allow_small_or_imprecise_dtypes=True))
+    need("v", tvf)
+    done("v", V.tensor_scalar(T.pa[:], T.pi[:], 112, None, AND))
+    done("v", V.tensor_scalar(T.pb[:], T.pi[:], 16, None, AND))
+    t = done("v", V.tensor_scalar(T.pc[:], T.pi[:], CH - 1, None, AND))
+    need("v", t)
+    done("v", V.tensor_copy(T.g16[:], T.pa[:]))
+    done("v", V.tensor_scalar(T.hi[:], T.pb[:], 0.0625, None, MUL))
+    done("v", V.tensor_scalar(T.lo[:], T.pb[:], -0.0625, 1.0, MUL, ADD))
+    t = done("v", V.tensor_scalar(T.run0[:], T.pc[:], -256.0, None, ADD))
+    need("v", t)
+    tva = done("v", V.tensor_scalar(T.vals[:], T.vfree[:], T.g16[:], None, ADD))
+
+    need("v", tu)
+    t = done("v", V.tensor_copy(T.ut[:, 0:4], T.usm[:]))
+    need("v", t)
+    t = done("v", V.quantize_mx(T.uq[:], T.up[:], T.ut[:]))
+    need("v", t)
+    done("v", V.tensor_copy(T.urq[:].bitcast(dt.uint32), T.uq[:].bitcast(dt.uint32).indirect(T.zoff[:])))
+    tur = done("v", V.tensor_copy(T.urp[:], T.up[:].indirect(T.zoff[:])))
+
+    def quant(c):
+        need("v", tx[c])
+        a, b = 128 * c, 128 * c + 128
+        return done("v", V.quantize_mx(T.xq[:, a:b], T.xp[:, a:b], T.xt[:, 4 * a:4 * b]))
+
+    def row(ps, q, p, a, b, *toks):
+        need("t", tur, *toks)
+        return done("t", P.matmul_mx(ps[:, 0:b - a], T.urq[:], T.urp[:], q[:, a:b], p[:, a:b], True, True))
+
+    def col(ps, q, p, a, *toks):
+        need("t", tur, *toks)
+        return done("t", P.matmul_mx(ps[:, 0:128], q[:, a:a + 128], p[:, a:a + 128], T.urq[:], T.urp[:], True, True))
+
+    def compact(dst, src, k, n, tok):
+        need("s", tok)
+        for a in range(4):
+            r = slice(32 * a, 32 * a + 32)
+            tk = done("s", S.activation(dst[r, k:k + n], src[r, 32 * a:32 * a + 128 * (n - 1) + 1:128], Copy))
+        return tk
+
+    RA, RB, P3 = T.ps0, T.ps1, T.ps2
+    quant(0)
+    t1 = quant(1)
+    tra = row(RA, T.xq, T.xp, 0, 256, t1)
+    quant(2)
+    need("v", tra)
+    for a in range(4):
+        r = slice(32 * a, 32 * a + 32)
+        tp0 = done("v", V.transpose(T.ss0[r, 0:32], RA[r, 32 * a:32 * a + 32]))
+    t1 = done("v", V.transpose(T.tt1[:], RA[:, 128:256]))
+    t3 = quant(3)
+    trb = row(RB, T.xq, T.xp, 256, 512, t3)
+    tp3 = col(P3, T.xq, T.xp, 384)
+    thr = [None] * 4
+
+    def threshold(b, ppc, tok):
+        need("s", tok)
+        tk = done("s", S.activation(T.dl[:, b:b + 1], ppc, Abs, bias=2.0 ** -120, scale=0.6 * 2.0 ** -23))
+        need("s", tk, tmk)
+        return done("s", S.activation(T.thr[:, 128 * b:128 * b + 128], T.mk[:], Ident, bias=ppc, scale=T.dl[:, b:b + 1]))
+
+    C0 = T.ss0[:, 0:1]
+    thr[0] = threshold(0, C0, tp0)
+    tp1 = compact(T.pp, T.tt1, 1, 1, t1)
+    thr[1] = threshold(1, T.pp[:, 1:2], tp1)
+
+    def cmp1(b, rw, c0, n, at, sc, op):
+        return done("v", V.tensor_scalar(T.cmp[:, 512 * b + at:512 * b + at + n], rw[:, c0:c0 + n], sc, None, op))
+
+    def diag1(b, rw, c0, at):
+        need("v", thr[b])
+        return done("v", V.tensor_tensor(T.cmp[:, 512 * b + at:512 * b + at + 128], rw[:, c0:c0 + 128],
+                                         T.thr[:, 128 * b:128 * b + 128], GT))
+
+    def scan1(b, tok):
+        need("v", tok)
+        o = 512 * b
+        return done("v", V.tensor_tensor_scan(T.so[:, 256 * b:256 * b + 256], T.cmp[:, o:o + 256],
+                                              T.cmp[:, o + 256:o + 512], -256.0, ADD, ADD))
+
+    need("v", tp0)
+    cmp1(0, RA, 128, 128, 128, C0, GT)
+    need("v", trb)
+    t2 = done("v", V.transpose(T.tt2[:], RB[:, 0:128]))
+    tp2 = compact(T.pp, T.tt2, 2, 1, t2)
+    need("s", tp3)
+    tp3 = done("s", S.activation(T.pp[:, 3:4], P3[:, 0:1], Copy))
+    thr[2] = threshold(2, T.pp[:, 2:3], tp2)
+    thr[3] = threshold(3, T.pp[:, 3:4], tp3)
+    cmp1(0, RB, 0, 256, 256, C0, GT)
+    d0 = diag1(0, RA, 0, 0)
+    need("v", tp1)
+    cmp1(1, RA, 0, 128, 0, T.pp[:, 1:2], GE)
+    cmp1(1, RB, 0, 256, 256, T.pp[:, 1:2], GT)
+    scan1(0, d0)
+    d1 = diag1(1, RA, 128, 128)
+    need("v", tp2)
+    cmp1(2, RA, 0, 256, 0, T.pp[:, 2:3], GE)
+    cmp1(2, RB, 128, 128, 384, T.pp[:, 2:3], GT)
+    scan1(1, d1)
+    d2 = diag1(2, RB, 0, 256)
+    need("v", tp3)
+    cmp1(3, RA, 0, 256, 0, T.pp[:, 3:4], GE)
+    cmp1(3, RB, 0, 128, 256, T.pp[:, 3:4], GE)
+    d3 = diag1(3, RB, 128, 384)
+    scan1(2, d2)
+    tcount = scan1(3, d3)
+
+    Q = [slice(32 * a, 32 * a + 32) for a in range(4)]
+
+    def make_list(k, ends, tok):
+        pl, sw, tr, ya, g1, g2, g3 = [T[n + k] for n in ("pl", "sw", "tr", "ya", "g1", "g2", "g3")]
+        xm, xx, fo, zz, off = [T[n + k] for n in ("xm", "xx", "fo", "zz", "off")]
+        need("v", tok)
+        tk = done("v", V.tensor_scalar(pl[:], ends, 256.0, None, ADD))
+        need("v", tk, tsw[k], tva)
+        tk = done("v", V.tensor_copy(sw[:, 0:512].indirect(pl[:]), T.vals[:]))
+        need("v", tk)
+        tk = done("v", V.transpose(tr[:], sw[:]))
+        need("v", tk)
+        tk = done("v", V.tensor_tensor(ya[:], tr[:, 0:512:32], tr[:, 16:512:32], ADD))
+        need("v", tk)
+        done("v", V.tensor_tensor(g1[Q[0], :], ya[Q[0], :], ya[Q[1], :], ADD))
+        tk = done("v", V.tensor_tensor(g2[Q[0], :], ya[Q[2], :], ya[Q[3], :], ADD))
+        need("v", tk)
+        tk = done("v", V.tensor_tensor(g3[Q[0], :], g1[Q[0], :], g2[Q[0], :], ADD))
+        need("v", tk)
+        done("v", V.tensor_scalar(xm[Q[0], 0:32:2], g3[Q[0], :], T.lo[Q[0], :], None, MUL))
+        tk = done("v", V.tensor_scalar(xm[Q[0], 1:32:2], g3[Q[0], :], T.hi[Q[0], :], None, MUL))
+        need("v", tk)
+        tk = done("v", V.transpose(xx[Q[0], :], xm[Q[0], :]))
+        need("v", tk)
+        done("v", V.tensor_tensor(fo[Q[0], 0:16], xx[Q[0], 0:16], xx[Q[0], 16:32], ADD))
+        tf = done("v", V.tensor_tensor(fo[Q[0], 16:32], xx[Q[0], 0:16], xx[Q[0], 16:32], ADD))
+        need("v", tf)
+        tk = done("v", V.transpose(zz[Q[0], :], fo[Q[0], :]))
+        need("v", tk)
+        for a in range(4):
+            tk = done("v", V.tensor_scalar(off[Q[a], :], zz[Q[0], :], 256.0, None, ADD))
+        return tf, tk
+
+    tfo, tof = make_list("a", T.so[:, 255:1024:256], tcount)
+
+    need("v", tof)
+    need("s", tof)
+    kc, ks = CH // 16, CH
+
+    def picks(dq, dp, sq, sp, off, a, b):
+        tv = done("v", V.tensor_copy(dq[:, a:b].bitcast(dt.uint32), sq[:].bitcast(dt.uint32).indirect(off[:, a // 16:b // 16])))
+        ts = done("s", S.activation(dp[:, a:b], sp[:].indirect(off[:, a // 16:b // 16]), Copy))
+        return tv, ts
+
+    tv = ts = None
+    for a, b in ((0, CH * me), (CH * (me + 1), 512)):
+        while a < b:
+            e = min(b, a + 512)
+            tv, ts = picks(T.slotq, T.slotp, T.xq, T.xp, T.offa, a, e)
+            a = e
+    ov, osc = picks(T.landq, T.landp, T.xq, T.xp, T.offa, CH * me, CH * me + CH)
+
+    others = [d for d in range(N) if d != me]
+    far = [d for d in others if topo.die(CORES[d]) != topo.die(core)]
+    near = [d for d in others if d not in far]
+    masks = {}
+    for grp, first in ((far, 0), (near, 1)):
+        for i, d in enumerate(grp):
+            el = topo.engines(core, CORES[d])
+            masks[d] = (1 << el[(4 * i + first) % len(el)]) | (1 << el[(4 * i + first + 2) % len(el)])
+    order = [others[(i + me) % len(others)] for i in range(len(others))]
+
+    def send(src, dst, sem):
+        tl = []
+        for d in order:
+            rid, pid, _s = topo.addr(CORES[d])
+            tl.append(RemoteDMATransfer(dst_ids=[DstId(rid=rid, pnc=pid)], dma_engine_mask=masks[d],
+                                        remote_sem=T.sem[sem], src=src(d), dst=dst))
+        g.remote_dma_fused(tl, local_sem=T.sem.ls)
+        cnt["ls"] = cnt.get("ls", 0) + 2 * len(others)
+
+    here = slice(CH * me, CH * me + CH)
+    half = "ara" if me < N // 2 else "arb"
+    need("g", tv)
+    send(lambda d: T.slotq[:, CH * d:CH * d + CH].bitcast(dt.uint8), T.landq[:, here].bitcast(dt.uint8), half)
+    need("g", ts)
+    send(lambda d: T.slotp[:, CH * d:CH * d + CH], T.landp[:, here], half)
+    need("s", tfo)
+    tcf = done("s", S.activation(T.colf[:], T.foa[Q[0], 0:16], Ident, bias=256.0))
+    need("y", tcf)
+    dma("dc", Y.dma_start(T.ocol[:], T.colf[:]))
+    tdc = dma("dc", Y.dma_start(T.rcol[me], T.colf[:]))
+    need("g", tdc)
+    send(lambda d: T.ocol[:], T.rcol[me], "arc")
+    need("y", tdc, ("arc", 2 * (N - 1)), tcr)
+    tdr = dma("dr", Y.dma_start(T.cr[1:2, :], T.rcol[:, CH // 4 * me:CH // 4 * me + CH // 4, :]))
+
+    need("v", tw)
+    twq = done("v", V.quantize_mx(T.wq[:], T.wp[:], T.wt[:]))
+
+    lo_n = 4 * (N // 2 - (1 if me < N // 2 else 0))
+    hi_n = 4 * (N // 2 - (0 if me < N // 2 else 1))
+    SA, SB, P0 = T.ps3, T.ps4, T.ps5
+    tsa = row(SA, T.landq, T.landp, 0, 256, ("ara", lo_n), *((ov, osc) if me < N // 2 else ()))
+    tq0 = col(P0, T.landq, T.landp, 0)
+    tsb = row(SB, T.landq, T.landp, 256, 512, ("arb", hi_n), ov, osc)
+
+    def cmp2(b, r, rw, c0, n, at, sc, op):
+        return done("v", V.tensor_scalar(T.cmq[r, 448 * b + at:448 * b + at + n], rw[r, c0:c0 + n], sc[r, :], None, op))
+
+    ALL, LO, HI = slice(0, 128), slice(0, 64), slice(64, 128)
+
+    def pair(b, rw, c0, sc):
+        cmp2(b, LO, rw, c0 + 64, 64, 0, sc, GT)
+        return cmp2(b, HI, rw, c0, 64, 0, sc, GE)
+
+    def scan2(b, tok):
+        need("v", tok)
+        o = 448 * b
+        return done("v", V.tensor_tensor_scan(T.sq[:, 224 * b:224 * b + 224], T.cmq[:, o:o + 224],
+                                              T.cmq[:, o + 224:o + 448], T.run0[:], ADD, ADD))
+
+    need("v", tsa)
+    t1 = done("v", V.transpose(T.ut1[:], SA[:, 128:256]))
+    tq1 = compact(T.qp, T.ut1, 1, 1, t1)
+    c0, c1, c2, c3 = P0[:, 0:1], T.qp[:, 1:2], T.qp[:, 2:3], T.qp[:, 3:4]
+    need("v", tq0)
+    pair(0, SA, 0, P0[:, 0:1])
+    cmp2(0, ALL, SA, 128, 128, 64, c0, GT)
+    need("v", tsb)
+    t2 = done("v", V.transpose(T.ut2[:], SB[:, 0:256]))
+    tq2 = compact(T.qp, T.ut2, 2, 2, t2)
+    e0 = cmp2(0, ALL, SB, 0, 256, 192, c0, GT)
+    need("v", tq1)
+    pair(1, SA, 128, c1)
+    cmp2(1, ALL, SA, 0, 128, 64, c1, GE)
+    e1 = cmp2(1, ALL, SB, 0, 256, 192, c1, GT)
+    scan2(0, e0)
+    need("v", tq2)
+    pair(2, SB, 0, c2)
+    cmp2(2, ALL, SB, 128, 128, 64, c2, GT)
+    e2 = cmp2(2, ALL, SA, 0, 256, 192, c2, GE)
+    scan2(1, e1)
+    pair(3, SB, 128, c3)
+    cmp2(3, ALL, SB, 0, 128, 64, c3, GE)
+    e3 = cmp2(3, ALL, SA, 0, 256, 192, c3, GE)
+    scan2(2, e2)
+    tcount = scan2(3, e3)
+    _f, tof = make_list("b", T.sq[:, 223:896:224], tcount)
+
+    need("v", tof)
+    need("s", tof)
+    YP = (T.ps6, T.ps7, T.ps0, T.ps1)
+    ty = []
+    for k in range(4):
+        a, b = 128 * k, 128 * k + 128
+        tv, ts = picks(T.finq, T.finp, T.landq, T.landp, T.offb, a, b)
+        need("t", twq, tv, ts)
+        ty.append(done("t", P.matmul_mx(YP[k][:, 0:128], T.wq[:, a:b], T.wp[:, a:b], T.finq[:, a:b], T.finp[:, a:b], True, True)))
+    for k in range(4):
+        a, b = 128 * k, 128 * k + 128
+        if k % 2 == 0:
+            need("v", ty[k])
+            tk = done("v", V.tensor_copy(T.yb[:, a:b], YP[k][:, 0:128]))
+        else:
+            need("s", ty[k])
+            tk = done("s", S.activation(T.yb[:, a:b], YP[k][:, 0:128], Copy))
+        need("y", tk)
+        dma("dy", Y.dma_start(T.y[:, a:b], T.yb[:, a:b]))
+    need("v", tdr)
+    ti1 = done("v", V.tensor_copy(T.idb[:, 0:256], T.cr[:].indirect(T.offb[:, 0:16])))
+    need("s", tdr)
+    ti2 = done("s", S.activation(T.idb[:, 256:512], T.cr[:].indirect(T.offb[:, 16:32]), Copy))
+    need("s", ti1, ti2)
+    dma("di", S.dma_start(T.ids[:], T.idb[0:2, :]))
+
+    for sem in ("cv", "cs", "ct", "cg", "dw", "dy", "di", "ls"):
+        need("g", (sem, cnt[sem]))

@@ -13,37 +13,29 @@ SCRATCH = {
     "slotq": ("sbuf", [128, 512], CODE), "slotp": ("sbuf", [128, 512], PLANE),
     "landq": ("sbuf", [128, 512], CODE), "landp": ("sbuf", [128, 512], PLANE),
     "finq": ("sbuf", [128, 512], CODE), "finp": ("sbuf", [128, 512], PLANE),
-    "zoff": ("sbuf", [128, 8], U16), "mk1": ("sbuf", [128, 128], F32), "mk": ("sbuf", [128, 128], F32),
+    "zoff": ("sbuf", [128, 8], U16), "colidx": ("sbuf", [128, 256], F32),
+    "mk0": ("sbuf", [128, 256], F32), "mk1": ("sbuf", [128, 256], F32),
     "pi": ("sbuf", [128, 1], I32), "pa": ("sbuf", [128, 1], I32), "pb": ("sbuf", [128, 1], I32),
-    "pc": ("sbuf", [128, 1], I32), "g16": ("sbuf", [128, 1], F32), "hi": ("sbuf", [128, 1], F32),
-    "lo": ("sbuf", [128, 1], F32), "run0": ("sbuf", [128, 1], F32), "vfree": ("sbuf", [128, 64], F32),
-    "vals": ("sbuf", [128, 64], BF),
-    "ss0": ("sbuf", [128, 32], F32), "tt1": ("sbuf", [128, 128], F32), "tt2": ("sbuf", [128, 128], F32),
-    "pp": ("sbuf", [128, 4], F32), "dl": ("sbuf", [128, 4], F32), "thr": ("sbuf", [128, 512], F32),
-    "cmp": ("sbuf", [128, 2048], BF), "so": ("sbuf", [128, 1024], BF),
-    "ut1": ("sbuf", [128, 128], F32), "ut2": ("sbuf", [128, 256], F32), "qp": ("sbuf", [128, 4], F32),
-    "cmq": ("sbuf", [128, 1792], BF), "sq": ("sbuf", [128, 896], BF),
-    "colf": ("sbuf", [32, 16], F32), "ocol": ("dram", [128, 4], F32), "rcol": ("dram", [8, 128, 4], F32),
+    "pf": ("sbuf", [128, 1], F32), "paf": ("sbuf", [128, 1], F32), "pbf": ("sbuf", [128, 1], F32),
+    "tc0": ("sbuf", [128, 1], F32), "tc1": ("sbuf", [128, 1], F32), "g64": ("sbuf", [128, 1], F32),
+    "vfree": ("sbuf", [128, 64], F32), "vals": ("sbuf", [128, 64], BF),
+    "colf": ("sbuf", [32, 32], F32), "ocol": ("dram", [128, 4], F32), "rcol": ("dram", [8, 128, 4], F32),
     "cr": ("sbuf", [128, 512], F32), "idb": ("sbuf", [128, 512], F32), "yb": ("sbuf", [128, 512], F32),
 }
 for _k in "ab":
-    SCRATCH["pl" + _k] = ("sbuf", [128, 4], U16)
-    SCRATCH["sw" + _k] = ("sbuf", [128, 512], BF)
-    SCRATCH["tr" + _k] = ("sbuf", [128, 512], BF)
-    SCRATCH["ya" + _k] = ("sbuf", [128, 16], BF)
-    SCRATCH["g1" + _k] = ("sbuf", [128, 16], BF)
-    SCRATCH["g2" + _k] = ("sbuf", [128, 16], BF)
-    SCRATCH["g3" + _k] = ("sbuf", [128, 16], BF)
-    SCRATCH["xm" + _k] = ("sbuf", [128, 32], BF)
-    SCRATCH["xx" + _k] = ("sbuf", [128, 32], BF)
-    SCRATCH["fo" + _k] = ("sbuf", [128, 32], BF)
-    SCRATCH["zz" + _k] = ("sbuf", [128, 32], BF)
-    SCRATCH["off" + _k] = ("sbuf", [128, 32], U16)
+    for _n, _w, _d in (("sa", 64, F32), ("sb", 64, F32), ("dl", 4, F32), ("thr", 1024, F32), ("cmp", 2048, BF),
+                       ("rel", 512, BF), ("sgn", 512, BF), ("nlt", 8, F32), ("so", 1024, BF),
+                       ("pl", 4, U16), ("sw", 512, BF), ("tr", 512, BF), ("ya", 32, BF), ("yt", 32, BF),
+                       ("za", 32, BF), ("zb", 32, BF), ("uu", 64, BF), ("vt", 64, BF), ("off", 32, U16)):
+        SCRATCH[_n + _k] = ("sbuf", [128, _w], _d)
 for _k in range(8):
     SCRATCH["ps%d" % _k] = ("psum", [128, 512], F32)
 
-SEMAPHORES = ["cv", "cs", "ct", "cg", "du", "dx0", "dx1", "dx2", "dx3", "dw", "dc", "dr", "dy", "di",
+SEMAPHORES = ["cv", "cs", "ct", "cg", "du", "dx0", "dx1", "dw", "dc", "dr", "dy", "di",
               "ara", "arb", "arc", "ls"]
+
+PLAN = {"va": "T0 q1 t0 T1 i0 x2 i1 x0 x1 i2 z0 z1 i3 z2 z3", "sa": "d0 t1 d1 t2 r3 t3 s3",
+        "vb": "T0 T1 x1 t1 x2 x0 i0 i2 i1 z0 z2 i3 z1 z3", "sb": "d0 d1 t0 t2 r3 t3 s3"}
 
 
 def rank_program(g, core, T, topo):
@@ -51,9 +43,10 @@ def rank_program(g, core, T, topo):
     if me is None:
         return
     V, S, P, Y = g.vector, g.scalar, g.tensor, g.sync
-    Copy, Ident, Abs = ActivationFunctionType.Copy, ActivationFunctionType.Identity, ActivationFunctionType.Abs
-    GT, GE, ADD, MUL = AluOpType.is_gt, AluOpType.is_ge, AluOpType.add, AluOpType.mult
-    AND = AluOpType.bitwise_and
+    AF = ActivationFunctionType
+    Copy, Ident = AF.Copy, AF.Identity
+    GT, GE, LT = AluOpType.is_gt, AluOpType.is_ge, AluOpType.is_lt
+    ADD, MUL, AND = AluOpType.add, AluOpType.mult, AluOpType.bitwise_and
     cnt, seen = {}, {}
     queue = {"v": V, "s": S, "t": P, "g": g, "y": Y}
     CORES = T.cores
@@ -78,181 +71,178 @@ def rank_program(g, core, T, topo):
         return (sem, cnt[sem])
 
     tu = dma("du", S.dma_start(T.usm[:], T.u[:, 0:4]))
-    tx = [None] * 4
-    for c in range(4):
-        tx[c] = dma("dx%d" % c, (Y, S)[c % 2].dma_start(T.xt[:, 512 * c:512 * c + 512], T.x[:, 512 * c:512 * c + 512]))
+    tx = [dma("dx0", Y.dma_start(T.xt[:, 0:1024], T.x[:, 0:1024])),
+          dma("dx1", S.dma_start(T.xt[:, 1024:2048], T.x[:, 1024:2048]))]
     need("y", *tx)
     dma("dw", Y.dma_start(T.wt[:, 0:1024], T.w[:, 0:1024]))
     tw = dma("dw", Y.dma_start(T.wt[:, 1024:2048], T.w[:, 1024:2048]))
 
-    tpi = done("g", g.iota(T.pi[:], [[1, 1]], 0, 1))
-    tvf = done("g", g.iota(T.vfree[:], [[128, 4], [1, 16]], -256, 0, allow_small_or_imprecise_dtypes=True))
-    tut = done("v", V.memset(T.ut[:], 0.0))
-    tzo = done("v", V.memset(T.zoff[:], 0))
-    tm1 = done("v", V.memset(T.mk1[:], -1.0))
-    tsw = {"a": done("v", V.memset(T.swa[:], 0.0)), "b": done("v", V.memset(T.swb[:], 0.0))}
-    need("g", tm1)
-    tmk = done("g", g.affine_select(T.mk[:], T.mk1[:], [[-1, 128]], GT, 0.0, 0, 1))
+    done("g", g.iota(T.pi[:], [[1, 1]], 0, 1))
+    tci = done("g", g.iota(T.colidx[:], [[1, 256]], 0, 0, allow_small_or_imprecise_dtypes=True))
+    tvf = done("g", g.iota(T.vfree[:], [[256, 2], [32, 2], [1, 16]], -256, 0, allow_small_or_imprecise_dtypes=True))
     tcr = done("g", g.iota(T.cr[:], [[1, N], [0, CH]], 0, 0, allow_small_or_imprecise_dtypes=True))
+    done("v", V.memset(T.ut[:], 0.0))
+    done("v", V.memset(T.zoff[:], 0))
+    done("v", V.memset(T.swa[:], 0.0))
+    done("v", V.memset(T.yaa[:, 16:32], 0.0))
+    done("v", V.memset(T.yab[:, 16:32], 0.0))
+    need("v", tci)
+    done("v", V.tensor_copy(T.pf[:], T.pi[:]))
+    done("v", V.tensor_scalar(T.pa[:], T.pi[:], 96, None, AND))
+    t = done("v", V.tensor_scalar(T.pb[:], T.pi[:], 16, None, AND))
+    need("v", t)
+    done("v", V.tensor_copy(T.paf[:], T.pa[:]))
+    t = done("v", V.tensor_copy(T.pbf[:], T.pb[:]))
+    need("v", t)
+    done("v", V.tensor_tensor(T.tc0[:], T.pf[:], T.paf[:], ADD))
+    t = done("v", V.tensor_scalar(T.g64[:], T.paf[:], 2.0, T.pbf[:], MUL, ADD))
+    need("v", t)
+    t = done("v", V.tensor_scalar(T.tc1[:], T.tc0[:], 32.0, None, ADD))
+    need("v", t)
+    MK = (T.mk0, T.mk1)
+    done("v", V.tensor_scalar(T.mk0[:], T.colidx[:], T.tc0[:], -1.0, LT, MUL))
+    tmk = done("v", V.tensor_scalar(T.mk1[:], T.colidx[:], T.tc1[:], -1.0, LT, MUL))
     need("v", tvf)
-    done("v", V.tensor_scalar(T.pa[:], T.pi[:], 112, None, AND))
-    done("v", V.tensor_scalar(T.pb[:], T.pi[:], 16, None, AND))
-    t = done("v", V.tensor_scalar(T.pc[:], T.pi[:], CH - 1, None, AND))
-    need("v", t)
-    done("v", V.tensor_copy(T.g16[:], T.pa[:]))
-    done("v", V.tensor_scalar(T.hi[:], T.pb[:], 0.0625, None, MUL))
-    done("v", V.tensor_scalar(T.lo[:], T.pb[:], -0.0625, 1.0, MUL, ADD))
-    t = done("v", V.tensor_scalar(T.run0[:], T.pc[:], -256.0, None, ADD))
-    need("v", t)
-    tva = done("v", V.tensor_scalar(T.vals[:], T.vfree[:], T.g16[:], None, ADD))
+    done("v", V.tensor_scalar(T.vals[:], T.vfree[:], T.g64[:], None, ADD))
 
     need("v", tu)
     t = done("v", V.tensor_copy(T.ut[:, 0:4], T.usm[:]))
     need("v", t)
     t = done("v", V.quantize_mx(T.uq[:], T.up[:], T.ut[:]))
     need("v", t)
-    done("v", V.tensor_copy(T.urq[:].bitcast(dt.uint32), T.uq[:].bitcast(dt.uint32).indirect(T.zoff[:])))
-    tur = done("v", V.tensor_copy(T.urp[:], T.up[:].indirect(T.zoff[:])))
+    tur = done("v", V.tensor_copy(T.urq[:].bitcast(dt.uint32), T.uq[:].bitcast(dt.uint32).indirect(T.zoff[:])))
+    need("s", t)
+    tup = done("s", S.activation(T.urp[:], T.up[:].indirect(T.zoff[:]), Copy))
 
-    def quant(c):
-        need("v", tx[c])
-        a, b = 128 * c, 128 * c + 128
-        return done("v", V.quantize_mx(T.xq[:, a:b], T.xp[:, a:b], T.xt[:, 4 * a:4 * b]))
-
-    def row(ps, q, p, a, b, *toks):
-        need("t", tur, *toks)
-        return done("t", P.matmul_mx(ps[:, 0:b - a], T.urq[:], T.urp[:], q[:, a:b], p[:, a:b], True, True))
-
-    def col(ps, q, p, a, *toks):
-        need("t", tur, *toks)
-        return done("t", P.matmul_mx(ps[:, 0:128], q[:, a:a + 128], p[:, a:a + 128], T.urq[:], T.urp[:], True, True))
-
-    def compact(dst, src, k, n, tok):
-        need("s", tok)
-        for a in range(4):
-            r = slice(32 * a, 32 * a + 32)
-            tk = done("s", S.activation(dst[r, k:k + n], src[r, 32 * a:32 * a + 128 * (n - 1) + 1:128], Copy))
-        return tk
-
-    RA, RB, P3 = T.ps0, T.ps1, T.ps2
-    quant(0)
-    t1 = quant(1)
-    tra = row(RA, T.xq, T.xp, 0, 256, t1)
-    quant(2)
-    need("v", tra)
-    for a in range(4):
-        r = slice(32 * a, 32 * a + 32)
-        tp0 = done("v", V.transpose(T.ss0[r, 0:32], RA[r, 32 * a:32 * a + 32]))
-    t1 = done("v", V.transpose(T.tt1[:], RA[:, 128:256]))
-    t3 = quant(3)
-    trb = row(RB, T.xq, T.xp, 256, 512, t3)
-    tp3 = col(P3, T.xq, T.xp, 384)
-    thr = [None] * 4
-
-    def threshold(b, ppc, tok):
-        need("s", tok)
-        tk = done("s", S.activation(T.dl[:, b:b + 1], ppc, Abs, bias=2.0 ** -120, scale=0.6 * 2.0 ** -23))
-        need("s", tk, tmk)
-        return done("s", S.activation(T.thr[:, 128 * b:128 * b + 128], T.mk[:], Ident, bias=ppc, scale=T.dl[:, b:b + 1]))
-
-    C0 = T.ss0[:, 0:1]
-    thr[0] = threshold(0, C0, tp0)
-    tp1 = compact(T.pp, T.tt1, 1, 1, t1)
-    thr[1] = threshold(1, T.pp[:, 1:2], tp1)
-
-    def cmp1(b, rw, c0, n, at, sc, op):
-        return done("v", V.tensor_scalar(T.cmp[:, 512 * b + at:512 * b + at + n], rw[:, c0:c0 + n], sc, None, op))
-
-    def diag1(b, rw, c0, at):
-        need("v", thr[b])
-        return done("v", V.tensor_tensor(T.cmp[:, 512 * b + at:512 * b + at + 128], rw[:, c0:c0 + 128],
-                                         T.thr[:, 128 * b:128 * b + 128], GT))
-
-    def scan1(b, tok):
-        need("v", tok)
-        o = 512 * b
-        return done("v", V.tensor_tensor_scan(T.so[:, 256 * b:256 * b + 256], T.cmp[:, o:o + 256],
-                                              T.cmp[:, o + 256:o + 512], -256.0, ADD, ADD))
-
-    need("v", tp0)
-    cmp1(0, RA, 128, 128, 128, C0, GT)
-    need("v", trb)
-    t2 = done("v", V.transpose(T.tt2[:], RB[:, 0:128]))
-    tp2 = compact(T.pp, T.tt2, 2, 1, t2)
-    need("s", tp3)
-    tp3 = done("s", S.activation(T.pp[:, 3:4], P3[:, 0:1], Copy))
-    thr[2] = threshold(2, T.pp[:, 2:3], tp2)
-    thr[3] = threshold(3, T.pp[:, 3:4], tp3)
-    cmp1(0, RB, 0, 256, 256, C0, GT)
-    d0 = diag1(0, RA, 0, 0)
-    need("v", tp1)
-    cmp1(1, RA, 0, 128, 0, T.pp[:, 1:2], GE)
-    cmp1(1, RB, 0, 256, 256, T.pp[:, 1:2], GT)
-    scan1(0, d0)
-    d1 = diag1(1, RA, 128, 128)
-    need("v", tp2)
-    cmp1(2, RA, 0, 256, 0, T.pp[:, 2:3], GE)
-    cmp1(2, RB, 128, 128, 384, T.pp[:, 2:3], GT)
-    scan1(1, d1)
-    d2 = diag1(2, RB, 0, 256)
-    need("v", tp3)
-    cmp1(3, RA, 0, 256, 0, T.pp[:, 3:4], GE)
-    cmp1(3, RB, 0, 128, 256, T.pp[:, 3:4], GE)
-    d3 = diag1(3, RB, 128, 384)
-    scan1(2, d2)
-    tcount = scan1(3, d3)
-
+    H = (slice(0, 64), slice(64, 128))
     Q = [slice(32 * a, 32 * a + 32) for a in range(4)]
 
-    def make_list(k, ends, tok):
-        pl, sw, tr, ya, g1, g2, g3 = [T[n + k] for n in ("pl", "sw", "tr", "ya", "g1", "g2", "g3")]
-        xm, xx, fo, zz, off = [T[n + k] for n in ("xm", "xx", "fo", "zz", "off")]
+    def row(ps, q, p, a, b, *toks):
+        need("t", tur, tup, *toks)
+        return done("t", P.matmul_mx(ps[:, 0:b - a], T.urq[:], T.urp[:], q[:, a:b], p[:, a:b], True, True))
+
+    def own(k, c):
+        return T[("sa", "sb")[c // 2] + k][:, 32 * (c % 2):32 * (c % 2) + 1]
+
+    def count(k, R, RS, tok, second=None):
+        cm, so, th, dl, rel, sgn, nlt = [T[n + k] for n in ("cmp", "so", "thr", "dl", "rel", "sgn", "nlt")]
+        vplan = PLAN["v" + k].split()
+        plan = {"v": list(vplan), "s": PLAN["s" + k].split()}
+        tok = dict(tok)
+        front = ["i0", "i1"] + [x for x in vplan if x in ("x2", "x3")]
+
+        def deps(w):
+            c = int(w[1])
+            h = c // 2
+            return {"q": [], "T": ["R%d" % c], "d": ["T%d" % c], "t": ["d%d" % h], "i": ["t%d" % c],
+                    "x": ["T%d" % h, "R%d" % (1 - h)], "r": ["T%d" % h] + (front if RS is None else ["RS"]),
+                    "s": ["r%d" % c], "z": ["i%d" % c, ("x%d" if "x%d" % c in vplan else "s%d") % c]}[w[0]]
+
+        def emit(q, w):
+            c = int(w[1])
+            h, at, o = c // 2, 512 * c, 256 * (c % 2)
+            if w[0] == "q":
+                return second()
+            need(q, *[tok[x] for x in deps(w)])
+            if w[0] == "T":
+                for a in range(4):
+                    tk = done("v", V.transpose(T[("sa", "sb")[c] + k][Q[a], 0:64], R[c][Q[a], 64 * a:64 * a + 64]))
+                return tk
+            if w[0] == "d":
+                return done("s", S.activation(dl[:, 2 * c:2 * c + 2], T[("sa", "sb")[c] + k][:, 0:64:32], AF.Abs,
+                                              bias=2.0 ** -120, scale=0.6 * 2.0 ** -23))
+            if w[0] == "t":
+                need(q, tmk)
+                to = th[:, 256 * c:256 * c + 256]
+                if q == "s":
+                    return done("s", S.activation(to, MK[c % 2][:], Ident, bias=own(k, c), scale=dl[:, c:c + 1]))
+                return done("v", V.tensor_scalar(to, MK[c % 2][:], dl[:, c:c + 1], own(k, c), MUL, ADD))
+            if w[0] == "i":
+                return done("v", V.tensor_tensor(cm[:, at:at + 256], R[h][:, 0:256], th[:, 256 * c:256 * c + 256], GT))
+            if w[0] == "x":
+                return done("v", V.tensor_scalar(cm[:, at + 256:at + 512], R[1 - h][:, 0:256], own(k, c), None, (GT, GE)[h]))
+            if w[0] == "r":
+                src = R[0] if RS is None else RS
+                return done("s", S.activation(rel[:, o:o + 256], src[:, 0:256], AF.Relu, bias=own(k, c), scale=-1.0))
+            if w[0] == "s":
+                return done("s", S.activation(sgn[:, o:o + 256], rel[:, o:o + 256], AF.Sign, scale=-1.0,
+                                              accum_out=nlt[:, 4 * (c % 2):4 * (c % 2) + 1]))
+            if "x%d" % c in vplan:
+                return done("v", V.tensor_tensor_scan(so[:, 256 * c:256 * c + 256], cm[:, at:at + 256], cm[:, at + 256:at + 512],
+                                                      -256.0, ADD, ADD))
+            return done("v", V.tensor_tensor_scan(so[:, 256 * c + 128:256 * c + 256], cm[:, at:at + 128], cm[:, at + 128:at + 256],
+                                                  nlt[:, 4 * (c % 2):4 * (c % 2) + 1], ADD, ADD))
+
+        while plan["v"] or plan["s"]:
+            for q in "vs":
+                while plan[q] and all(x in tok for x in deps(plan[q][0])):
+                    w = plan[q].pop(0)
+                    tok["R1" if w == "q1" else w] = emit(q, w)
+        return tok[vplan[-1]]
+
+    def make_list(k, tok):
+        pl, sw, tr, ya, yt, za, zb, uu, vt, off = [T[n + k] for n in ("pl", "sw", "tr", "ya", "yt", "za", "zb", "uu", "vt", "off")]
         need("v", tok)
-        tk = done("v", V.tensor_scalar(pl[:], ends, 256.0, None, ADD))
-        need("v", tk, tsw[k], tva)
+        tk = done("v", V.tensor_scalar(pl[:], T["so" + k][:, 255:1024:256], 256.0, None, ADD))
+        need("v", tk)
         tk = done("v", V.tensor_copy(sw[:, 0:512].indirect(pl[:]), T.vals[:]))
         need("v", tk)
         tk = done("v", V.transpose(tr[:], sw[:]))
         need("v", tk)
-        tk = done("v", V.tensor_tensor(ya[:], tr[:, 0:512:32], tr[:, 16:512:32], ADD))
+        tk = done("v", V.tensor_tensor(ya[:, 0:16], tr[:, 0:512:32], tr[:, 16:512:32], ADD))
         need("v", tk)
-        done("v", V.tensor_tensor(g1[Q[0], :], ya[Q[0], :], ya[Q[1], :], ADD))
-        tk = done("v", V.tensor_tensor(g2[Q[0], :], ya[Q[2], :], ya[Q[3], :], ADD))
+        tk = done("v", V.transpose(yt[:], ya[:]))
         need("v", tk)
-        tk = done("v", V.tensor_tensor(g3[Q[0], :], g1[Q[0], :], g2[Q[0], :], ADD))
+        done("v", V.tensor_tensor(za[H[0], :], yt[H[0], :], yt[H[1], :], ADD))
+        for a in range(2):
+            tk = done("v", V.tensor_tensor(zb[Q[a], :], yt[Q[a ^ 1], :], yt[Q[a ^ 3], :], ADD))
         need("v", tk)
-        done("v", V.tensor_scalar(xm[Q[0], 0:32:2], g3[Q[0], :], T.lo[Q[0], :], None, MUL))
-        tk = done("v", V.tensor_scalar(xm[Q[0], 1:32:2], g3[Q[0], :], T.hi[Q[0], :], None, MUL))
+        for j in (1, 2, 0, 3):
+            h = 16 * (j // 2)
+            tk = done("v", V.tensor_tensor(uu[H[0], 16 * j:16 * j + 16], za[H[0], h:h + 16], zb[H[0], h:h + 16], ADD))
+            if j == 2:
+                tf = tk
         need("v", tk)
-        tk = done("v", V.transpose(xx[Q[0], :], xm[Q[0], :]))
+        tk = done("v", V.transpose(vt[H[0], :], uu[H[0], :]))
         need("v", tk)
-        done("v", V.tensor_tensor(fo[Q[0], 0:16], xx[Q[0], 0:16], xx[Q[0], 16:32], ADD))
-        tf = done("v", V.tensor_tensor(fo[Q[0], 16:32], xx[Q[0], 0:16], xx[Q[0], 16:32], ADD))
-        need("v", tf)
-        tk = done("v", V.transpose(zz[Q[0], :], fo[Q[0], :]))
-        need("v", tk)
-        for a in range(4):
-            tk = done("v", V.tensor_scalar(off[Q[a], :], zz[Q[0], :], 256.0, None, ADD))
+        for r in H:
+            done("v", V.tensor_scalar(off[r, 0:32:2], vt[H[0], 0:16], 256.0, None, ADD))
+            tk = done("v", V.tensor_scalar(off[r, 1:32:2], vt[H[0], 32:48], 256.0, None, ADD))
         return tf, tk
 
-    tfo, tof = make_list("a", T.so[:, 255:1024:256], tcount)
+    RA, RB = T.ps0, T.ps1
 
+    def quant(h):
+        need("v", tx[h])
+        a, b = 256 * h, 256 * h + 256
+        return done("v", V.quantize_mx(T.xq[:, a:b], T.xp[:, a:b], T.xt[:, 4 * a:4 * b]))
+
+    tra = row(RA, T.xq, T.xp, 0, 256, quant(0))
+    tcount = count("a", (RA, RB), None, {"R0": tra}, lambda: row(RB, T.xq, T.xp, 256, 512, quant(1)))
+    tfo, tof = make_list("a", tcount)
+
+    need("s", tfo)
+    tcf = done("s", S.activation(T.colf[:], T.uua[Q[0], 16:48], Ident, bias=256.0))
     need("v", tof)
     need("s", tof)
-    kc, ks = CH // 16, CH
 
-    def picks(dq, dp, sq, sp, off, a, b):
-        tv = done("v", V.tensor_copy(dq[:, a:b].bitcast(dt.uint32), sq[:].bitcast(dt.uint32).indirect(off[:, a // 16:b // 16])))
-        ts = done("s", S.activation(dp[:, a:b], sp[:].indirect(off[:, a // 16:b // 16]), Copy))
-        return tv, ts
+    def codes(dst, src, off, a, b):
+        return done("v", V.tensor_copy(dst[:, a:b].bitcast(dt.uint32), src[:].bitcast(dt.uint32).indirect(off[:, a // 16:b // 16])))
 
-    tv = ts = None
-    for a, b in ((0, CH * me), (CH * (me + 1), 512)):
-        while a < b:
-            e = min(b, a + 512)
-            tv, ts = picks(T.slotq, T.slotp, T.xq, T.xp, T.offa, a, e)
-            a = e
-    ov, osc = picks(T.landq, T.landp, T.xq, T.xp, T.offa, CH * me, CH * me + CH)
+    def scales(q, dst, src, off, a, b):
+        o, i = dst[:, a:b], src[:].indirect(off[:, a // 16:b // 16])
+        return done("s", S.activation(o, i, Copy)) if q == "s" else done("v", V.tensor_copy(o, i))
+
+    parts = []
+    for a in (0, 256):
+        b = a + 256
+        parts.append((a + CH if CH * me == a else a, b - CH if CH * me + CH == b else b))
+    tsv = scales("v", T.slotp, T.xp, T.offa, *parts[0])
+    tss = scales("s", T.slotp, T.xp, T.offa, *parts[1])
+    for a, b in parts:
+        tcode = codes(T.slotq, T.xq, T.offa, a, b)
+    ov = codes(T.landq, T.xq, T.offa, CH * me, CH * me + CH)
+    osc = scales("s", T.landp, T.xp, T.offa, CH * me, CH * me + CH)
 
     others = [d for d in range(N) if d != me]
     far = [d for d in others if topo.die(CORES[d]) != topo.die(core)]
@@ -275,72 +265,29 @@ def rank_program(g, core, T, topo):
 
     here = slice(CH * me, CH * me + CH)
     half = "ara" if me < N // 2 else "arb"
-    need("g", tv)
-    send(lambda d: T.slotq[:, CH * d:CH * d + CH].bitcast(dt.uint8), T.landq[:, here].bitcast(dt.uint8), half)
-    need("g", ts)
+    need("g", tsv, tss)
     send(lambda d: T.slotp[:, CH * d:CH * d + CH], T.landp[:, here], half)
-    need("s", tfo)
-    tcf = done("s", S.activation(T.colf[:], T.foa[Q[0], 0:16], Ident, bias=256.0))
+    need("g", tcode)
+    send(lambda d: T.slotq[:, CH * d:CH * d + CH].bitcast(dt.uint8), T.landq[:, here].bitcast(dt.uint8), half)
     need("y", tcf)
-    dma("dc", Y.dma_start(T.ocol[:], T.colf[:]))
-    tdc = dma("dc", Y.dma_start(T.rcol[me], T.colf[:]))
+    dma("dc", Y.dma_start(T.ocol[:], T.colf[0:16, :]))
+    tdc = dma("dc", Y.dma_start(T.rcol[me], T.colf[0:16, :]))
     need("g", tdc)
     send(lambda d: T.ocol[:], T.rcol[me], "arc")
     need("y", tdc, ("arc", 2 * (N - 1)), tcr)
     tdr = dma("dr", Y.dma_start(T.cr[1:2, :], T.rcol[:, CH // 4 * me:CH // 4 * me + CH // 4, :]))
 
+    done("v", V.memset(T.swb[:], 0.0))
     need("v", tw)
     twq = done("v", V.quantize_mx(T.wq[:], T.wp[:], T.wt[:]))
 
     lo_n = 4 * (N // 2 - (1 if me < N // 2 else 0))
     hi_n = 4 * (N // 2 - (0 if me < N // 2 else 1))
-    SA, SB, P0 = T.ps3, T.ps4, T.ps5
+    SA, SB, SC = T.ps3, T.ps4, T.ps5
     tsa = row(SA, T.landq, T.landp, 0, 256, ("ara", lo_n), *((ov, osc) if me < N // 2 else ()))
-    tq0 = col(P0, T.landq, T.landp, 0)
     tsb = row(SB, T.landq, T.landp, 256, 512, ("arb", hi_n), ov, osc)
-
-    def cmp2(b, r, rw, c0, n, at, sc, op):
-        return done("v", V.tensor_scalar(T.cmq[r, 448 * b + at:448 * b + at + n], rw[r, c0:c0 + n], sc[r, :], None, op))
-
-    ALL, LO, HI = slice(0, 128), slice(0, 64), slice(64, 128)
-
-    def pair(b, rw, c0, sc):
-        cmp2(b, LO, rw, c0 + 64, 64, 0, sc, GT)
-        return cmp2(b, HI, rw, c0, 64, 0, sc, GE)
-
-    def scan2(b, tok):
-        need("v", tok)
-        o = 448 * b
-        return done("v", V.tensor_tensor_scan(T.sq[:, 224 * b:224 * b + 224], T.cmq[:, o:o + 224],
-                                              T.cmq[:, o + 224:o + 448], T.run0[:], ADD, ADD))
-
-    need("v", tsa)
-    t1 = done("v", V.transpose(T.ut1[:], SA[:, 128:256]))
-    tq1 = compact(T.qp, T.ut1, 1, 1, t1)
-    c0, c1, c2, c3 = P0[:, 0:1], T.qp[:, 1:2], T.qp[:, 2:3], T.qp[:, 3:4]
-    need("v", tq0)
-    pair(0, SA, 0, P0[:, 0:1])
-    cmp2(0, ALL, SA, 128, 128, 64, c0, GT)
-    need("v", tsb)
-    t2 = done("v", V.transpose(T.ut2[:], SB[:, 0:256]))
-    tq2 = compact(T.qp, T.ut2, 2, 2, t2)
-    e0 = cmp2(0, ALL, SB, 0, 256, 192, c0, GT)
-    need("v", tq1)
-    pair(1, SA, 128, c1)
-    cmp2(1, ALL, SA, 0, 128, 64, c1, GE)
-    e1 = cmp2(1, ALL, SB, 0, 256, 192, c1, GT)
-    scan2(0, e0)
-    need("v", tq2)
-    pair(2, SB, 0, c2)
-    cmp2(2, ALL, SB, 128, 128, 64, c2, GT)
-    e2 = cmp2(2, ALL, SA, 0, 256, 192, c2, GE)
-    scan2(1, e1)
-    pair(3, SB, 128, c3)
-    cmp2(3, ALL, SB, 0, 128, 64, c3, GE)
-    e3 = cmp2(3, ALL, SA, 0, 256, 192, c3, GE)
-    scan2(2, e2)
-    tcount = scan2(3, e3)
-    _f, tof = make_list("b", T.sq[:, 223:896:224], tcount)
+    tsc = row(SC, T.landq, T.landp, 0, 256)
+    _f, tof = make_list("b", count("b", (SA, SB), SC, {"R0": tsa, "R1": tsb, "RS": tsc}))
 
     need("v", tof)
     need("s", tof)
@@ -348,23 +295,21 @@ def rank_program(g, core, T, topo):
     ty = []
     for k in range(4):
         a, b = 128 * k, 128 * k + 128
-        tv, ts = picks(T.finq, T.finp, T.landq, T.landp, T.offb, a, b)
+        if k % 2 == 0:
+            tv = codes(T.finq, T.landq, T.offb, a, a + 256)
+            ts = scales("s", T.finp, T.landp, T.offb, a, a + 256)
         need("t", twq, tv, ts)
         ty.append(done("t", P.matmul_mx(YP[k][:, 0:128], T.wq[:, a:b], T.wp[:, a:b], T.finq[:, a:b], T.finp[:, a:b], True, True)))
-    for k in range(4):
-        a, b = 128 * k, 128 * k + 128
-        if k % 2 == 0:
-            need("v", ty[k])
-            tk = done("v", V.tensor_copy(T.yb[:, a:b], YP[k][:, 0:128]))
-        else:
-            need("s", ty[k])
-            tk = done("s", S.activation(T.yb[:, a:b], YP[k][:, 0:128], Copy))
-        need("y", tk)
-        dma("dy", Y.dma_start(T.y[:, a:b], T.yb[:, a:b]))
+    for k in (0, 2):
+        for b in (k, k + 1):
+            need("v", ty[b])
+            t = done("v", V.tensor_copy(T.yb[:, 128 * b:128 * b + 128], YP[b][:, 0:128]))
+        need("y", t)
+        dma("dy", Y.dma_start(T.y[:, 128 * k:128 * k + 256], T.yb[:, 128 * k:128 * k + 256]))
     need("v", tdr)
-    ti1 = done("v", V.tensor_copy(T.idb[:, 0:256], T.cr[:].indirect(T.offb[:, 0:16])))
+    ti1 = done("v", V.tensor_copy(T.idb[:, 0:128], T.cr[:].indirect(T.offb[:, 0:8])))
     need("s", tdr)
-    ti2 = done("s", S.activation(T.idb[:, 256:512], T.cr[:].indirect(T.offb[:, 16:32]), Copy))
+    ti2 = done("s", S.activation(T.idb[:, 128:512], T.cr[:].indirect(T.offb[:, 8:32]), Copy))
     need("s", ti1, ti2)
     dma("di", S.dma_start(T.ids[:], T.idb[0:2, :]))
 

@@ -4,7 +4,7 @@ from concourse.mybir import dt, AluOpType, ActivationFunctionType
 F32, BF, I32, U16 = "float32", "bfloat16", "int32", "uint16"
 CODE, PLANE = "float8_e4m3fn_x4", "uint8"
 SCRATCH = {
-    "usm": ("sbuf", [128, 4], BF), "ut": ("sbuf", [128, 512], BF),
+    "ut": ("sbuf", [128, 512], BF),
     "xt": ("sbuf", [128, 2048], BF), "wt": ("sbuf", [128, 2048], BF),
     "uq": ("sbuf", [128, 128], CODE), "up": ("sbuf", [128, 128], PLANE),
     "urq": ("sbuf", [128, 128], CODE), "urp": ("sbuf", [128, 128], PLANE),
@@ -34,7 +34,7 @@ for _k in range(8):
 SEMAPHORES = ["cv", "cs", "ct", "cg", "du", "dx0", "dx1", "dw", "dc", "dr", "dy", "di",
               "ara", "arb", "arc", "ls"]
 
-PLAN = {"va": "T0 q1 t0 T1 i0 x2 i1 x0 x1 i2 z0 z1 i3 z2 z3", "sa": "d0 t1 d1 t2 r3 t3 s3",
+PLAN = {"va": "m0 T0 m1 q1 t0 T1 i0 x2 i1 x0 x1 i2 z0 z1 i3 z2 z3", "sa": "d0 t1 d1 t2 r3 t3 s3",
         "vb": "T0 T1 x1 t1 x2 x0 i0 i2 i1 z0 z2 i3 z1 z3", "sb": "d0 d1 t0 t2 r3 t3 s3"}
 
 
@@ -70,49 +70,52 @@ def rank_program(g, core, T, topo):
         cnt[sem] = cnt.get(sem, 0) + 16
         return (sem, cnt[sem])
 
-    tu = dma("du", S.dma_start(T.usm[:], T.u[:, 0:4]))
+    tu = dma("du", S.dma_start(T.ut[:, 0:8], T.u[:, 0:8]))
     tx = [dma("dx0", Y.dma_start(T.xt[:, 0:1024], T.x[:, 0:1024])),
           dma("dx1", S.dma_start(T.xt[:, 1024:2048], T.x[:, 1024:2048]))]
     need("y", *tx)
     dma("dw", Y.dma_start(T.wt[:, 0:1024], T.w[:, 0:1024]))
     tw = dma("dw", Y.dma_start(T.wt[:, 1024:2048], T.w[:, 1024:2048]))
 
-    done("g", g.iota(T.pi[:], [[1, 1]], 0, 1))
+    tpi = done("g", g.iota(T.pi[:], [[1, 1]], 0, 1))
+    tpf = done("g", g.iota(T.pf[:], [[1, 1]], 0, 1, allow_small_or_imprecise_dtypes=True))
     tci = done("g", g.iota(T.colidx[:], [[1, 256]], 0, 0, allow_small_or_imprecise_dtypes=True))
     tvf = done("g", g.iota(T.vfree[:], [[256, 2], [32, 2], [1, 16]], -256, 0, allow_small_or_imprecise_dtypes=True))
     tcr = done("g", g.iota(T.cr[:], [[1, N], [0, CH]], 0, 0, allow_small_or_imprecise_dtypes=True))
-    done("v", V.memset(T.ut[:], 0.0))
-    done("v", V.memset(T.zoff[:], 0))
-    done("v", V.memset(T.swa[:], 0.0))
-    done("v", V.memset(T.yaa[:, 16:32], 0.0))
-    done("v", V.memset(T.yab[:, 16:32], 0.0))
-    need("v", tci)
-    done("v", V.tensor_copy(T.pf[:], T.pi[:]))
+
+    done("v", V.memset(T.ut[:, 8:512], 0.0))
+    tz = done("v", V.memset(T.zoff[:], 0))
+    need("v", tpi)
     done("v", V.tensor_scalar(T.pa[:], T.pi[:], 96, None, AND))
     t = done("v", V.tensor_scalar(T.pb[:], T.pi[:], 16, None, AND))
+    done("v", V.memset(T.swa[:], 0.0))
     need("v", t)
     done("v", V.tensor_copy(T.paf[:], T.pa[:]))
-    t = done("v", V.tensor_copy(T.pbf[:], T.pb[:]))
-    need("v", t)
-    done("v", V.tensor_tensor(T.tc0[:], T.pf[:], T.paf[:], ADD))
-    t = done("v", V.tensor_scalar(T.g64[:], T.paf[:], 2.0, T.pbf[:], MUL, ADD))
-    need("v", t)
-    t = done("v", V.tensor_scalar(T.tc1[:], T.tc0[:], 32.0, None, ADD))
-    need("v", t)
-    MK = (T.mk0, T.mk1)
-    done("v", V.tensor_scalar(T.mk0[:], T.colidx[:], T.tc0[:], -1.0, LT, MUL))
-    tmk = done("v", V.tensor_scalar(T.mk1[:], T.colidx[:], T.tc1[:], -1.0, LT, MUL))
-    need("v", tvf)
-    done("v", V.tensor_scalar(T.vals[:], T.vfree[:], T.g64[:], None, ADD))
+    tpb = done("v", V.tensor_copy(T.pbf[:], T.pb[:]))
 
-    need("v", tu)
-    t = done("v", V.tensor_copy(T.ut[:, 0:4], T.usm[:]))
-    need("v", t)
-    t = done("v", V.quantize_mx(T.uq[:], T.up[:], T.ut[:]))
-    need("v", t)
+    need("v", tu, tz)
+    tq = done("v", V.quantize_mx(T.uq[:], T.up[:], T.ut[:]))
+    need("v", tpf, tpb)
+    done("v", V.tensor_tensor(T.tc0[:], T.pf[:], T.paf[:], ADD))
+    tg64 = done("v", V.tensor_scalar(T.g64[:], T.paf[:], 2.0, T.pbf[:], MUL, ADD))
+    need("v", tq)
     tur = done("v", V.tensor_copy(T.urq[:].bitcast(dt.uint32), T.uq[:].bitcast(dt.uint32).indirect(T.zoff[:])))
-    need("s", t)
+    need("s", tq, tz)
     tup = done("s", S.activation(T.urp[:], T.up[:].indirect(T.zoff[:]), Copy))
+    need("v", tg64)
+    ttc = done("v", V.tensor_scalar(T.tc1[:], T.tc0[:], 32.0, None, ADD))
+
+    MK = (T.mk0, T.mk1)
+    mkt = {}
+
+    def mask(i):
+        need("v", tci, ttc)
+        mkt[i] = done("v", V.tensor_scalar(MK[i][:], T.colidx[:], (T.tc0, T.tc1)[i][:], -1.0, LT, MUL))
+        if i == 1:
+            need("v", tvf)
+            done("v", V.tensor_scalar(T.vals[:], T.vfree[:], T.g64[:], None, ADD))
+            done("v", V.memset(T.yaa[:, 16:32], 0.0))
+        return mkt[i]
 
     H = (slice(0, 64), slice(64, 128))
     Q = [slice(32 * a, 32 * a + 32) for a in range(4)]
@@ -129,12 +132,13 @@ def rank_program(g, core, T, topo):
         vplan = PLAN["v" + k].split()
         plan = {"v": list(vplan), "s": PLAN["s" + k].split()}
         tok = dict(tok)
+        tok.update({"m%d" % i: mkt[i] for i in mkt})
         front = ["i0", "i1"] + [x for x in vplan if x in ("x2", "x3")]
 
         def deps(w):
             c = int(w[1])
             h = c // 2
-            return {"q": [], "T": ["R%d" % c], "d": ["T%d" % c], "t": ["d%d" % h], "i": ["t%d" % c],
+            return {"q": [], "m": [], "T": ["R%d" % c], "d": ["T%d" % c], "t": ["d%d" % h, "m%d" % (c % 2)], "i": ["t%d" % c],
                     "x": ["T%d" % h, "R%d" % (1 - h)], "r": ["T%d" % h] + (front if RS is None else ["RS"]),
                     "s": ["r%d" % c], "z": ["i%d" % c, ("x%d" if "x%d" % c in vplan else "s%d") % c]}[w[0]]
 
@@ -143,6 +147,8 @@ def rank_program(g, core, T, topo):
             h, at, o = c // 2, 512 * c, 256 * (c % 2)
             if w[0] == "q":
                 return second()
+            if w[0] == "m":
+                return mask(c)
             need(q, *[tok[x] for x in deps(w)])
             if w[0] == "T":
                 for a in range(4):
@@ -152,7 +158,6 @@ def rank_program(g, core, T, topo):
                 return done("s", S.activation(dl[:, 2 * c:2 * c + 2], T[("sa", "sb")[c] + k][:, 0:64:32], AF.Abs,
                                               bias=2.0 ** -120, scale=0.6 * 2.0 ** -23))
             if w[0] == "t":
-                need(q, tmk)
                 to = th[:, 256 * c:256 * c + 256]
                 if q == "s":
                     return done("s", S.activation(to, MK[c % 2][:], Ident, bias=own(k, c), scale=dl[:, c:c + 1]))
@@ -229,63 +234,71 @@ def rank_program(g, core, T, topo):
     def codes(dst, src, off, a, b):
         return done("v", V.tensor_copy(dst[:, a:b].bitcast(dt.uint32), src[:].bitcast(dt.uint32).indirect(off[:, a // 16:b // 16])))
 
-    def scales(q, dst, src, off, a, b):
-        o, i = dst[:, a:b], src[:].indirect(off[:, a // 16:b // 16])
-        return done("s", S.activation(o, i, Copy)) if q == "s" else done("v", V.tensor_copy(o, i))
+    def scales(dst, src, off, a, b):
+        return done("s", S.activation(dst[:, a:b], src[:].indirect(off[:, a // 16:b // 16]), Copy))
 
-    parts = []
-    for a in (0, 256):
-        b = a + 256
-        parts.append((a + CH if CH * me == a else a, b - CH if CH * me + CH == b else b))
-    tsv = scales("v", T.slotp, T.xp, T.offa, *parts[0])
-    tss = scales("s", T.slotp, T.xp, T.offa, *parts[1])
-    for a, b in parts:
-        tcode = codes(T.slotq, T.xq, T.offa, a, b)
+    def firsts(s):
+        return (N - 2, N - 1) if s < N // 2 else (0, 1)
+
+    lo, hi = (CH if me == 0 else 0), (512 - CH if me == N - 1 else 512)
+    fa, fb = CH * firsts(me)[0], CH * firsts(me)[1] + CH
+    rest = (lo, fa) if fa else (fb, hi)
+    tsc1 = scales(T.slotp, T.xp, T.offa, fa, fb)
+    tsc2 = scales(T.slotp, T.xp, T.offa, *rest)
+    codes(T.slotq, T.xq, T.offa, fa, fb)
+    tcode = codes(T.slotq, T.xq, T.offa, *rest)
     ov = codes(T.landq, T.xq, T.offa, CH * me, CH * me + CH)
-    osc = scales("s", T.landp, T.xp, T.offa, CH * me, CH * me + CH)
+    osc = scales(T.landp, T.xp, T.offa, CH * me, CH * me + CH)
 
     others = [d for d in range(N) if d != me]
     far = [d for d in others if topo.die(CORES[d]) != topo.die(core)]
     near = [d for d in others if d not in far]
-    masks = {}
+    masks, wide = {}, {}
     for grp, first in ((far, 0), (near, 1)):
         for i, d in enumerate(grp):
             el = topo.engines(core, CORES[d])
             masks[d] = (1 << el[(4 * i + first) % len(el)]) | (1 << el[(4 * i + first + 2) % len(el)])
+    for i, d in enumerate(firsts(me)):
+        wide[d] = sum(1 << e for e in topo.engines(core, CORES[d])[i::2])
+    NW = len(topo.engines(core, CORES[firsts(me)[0]])) // 2
     order = [others[(i + me) % len(others)] for i in range(len(others))]
 
-    def send(src, dst, sem):
+    def send(ds, eng, src, dst, sem):
         tl = []
-        for d in order:
+        for d in ds:
             rid, pid, _s = topo.addr(CORES[d])
-            tl.append(RemoteDMATransfer(dst_ids=[DstId(rid=rid, pnc=pid)], dma_engine_mask=masks[d],
+            tl.append(RemoteDMATransfer(dst_ids=[DstId(rid=rid, pnc=pid)], dma_engine_mask=eng[d],
                                         remote_sem=T.sem[sem], src=src(d), dst=dst))
         g.remote_dma_fused(tl, local_sem=T.sem.ls)
-        cnt["ls"] = cnt.get("ls", 0) + 2 * len(others)
+        cnt["ls"] = cnt.get("ls", 0) + len(ds) * (NW if eng is wide else 2)
 
     here = slice(CH * me, CH * me + CH)
     half = "ara" if me < N // 2 else "arb"
-    need("g", tsv, tss)
-    send(lambda d: T.slotp[:, CH * d:CH * d + CH], T.landp[:, here], half)
+    need("g", tsc1)
+    send(firsts(me), wide, lambda d: T.slotp[:, CH * d:CH * d + CH], T.landp[:, here], half)
     need("g", tcode)
-    send(lambda d: T.slotq[:, CH * d:CH * d + CH].bitcast(dt.uint8), T.landq[:, here].bitcast(dt.uint8), half)
+    send(order, masks, lambda d: T.slotq[:, CH * d:CH * d + CH].bitcast(dt.uint8), T.landq[:, here].bitcast(dt.uint8), half)
+    need("g", tsc2)
+    send([d for d in order if d not in firsts(me)], masks, lambda d: T.slotp[:, CH * d:CH * d + CH], T.landp[:, here], half)
     need("y", tcf)
     dma("dc", Y.dma_start(T.ocol[:], T.colf[0:16, :]))
     tdc = dma("dc", Y.dma_start(T.rcol[me], T.colf[0:16, :]))
     need("g", tdc)
-    send(lambda d: T.ocol[:], T.rcol[me], "arc")
+    send(order, masks, lambda d: T.ocol[:], T.rcol[me], "arc")
     need("y", tdc, ("arc", 2 * (N - 1)), tcr)
     tdr = dma("dr", Y.dma_start(T.cr[1:2, :], T.rcol[:, CH // 4 * me:CH // 4 * me + CH // 4, :]))
 
     done("v", V.memset(T.swb[:], 0.0))
+    done("v", V.memset(T.yab[:, 16:32], 0.0))
     need("v", tw)
     twq = done("v", V.quantize_mx(T.wq[:], T.wp[:], T.wt[:]))
 
-    lo_n = 4 * (N // 2 - (1 if me < N // 2 else 0))
-    hi_n = 4 * (N // 2 - (0 if me < N // 2 else 1))
+    def landed(ranks):
+        return sum(2 + (NW if me in firsts(s) else 2) for s in ranks if s != me)
+
     SA, SB, SC = T.ps3, T.ps4, T.ps5
-    tsa = row(SA, T.landq, T.landp, 0, 256, ("ara", lo_n), *((ov, osc) if me < N // 2 else ()))
-    tsb = row(SB, T.landq, T.landp, 256, 512, ("arb", hi_n), ov, osc)
+    tsa = row(SA, T.landq, T.landp, 0, 256, ("ara", landed(range(N // 2))), *((ov, osc) if me < N // 2 else ()))
+    tsb = row(SB, T.landq, T.landp, 256, 512, ("arb", landed(range(N // 2, N))), ov, osc)
     tsc = row(SC, T.landq, T.landp, 0, 256)
     _f, tof = make_list("b", count("b", (SA, SB), SC, {"R0": tsa, "R1": tsb, "RS": tsc}))
 
@@ -297,7 +310,7 @@ def rank_program(g, core, T, topo):
         a, b = 128 * k, 128 * k + 128
         if k % 2 == 0:
             tv = codes(T.finq, T.landq, T.offb, a, a + 256)
-            ts = scales("s", T.finp, T.landp, T.offb, a, a + 256)
+            ts = scales(T.finp, T.landp, T.offb, a, a + 256)
         need("t", twq, tv, ts)
         ty.append(done("t", P.matmul_mx(YP[k][:, 0:128], T.wq[:, a:b], T.wp[:, a:b], T.finq[:, a:b], T.finp[:, a:b], True, True)))
     for k in (0, 2):

from concourse.bass import DstId, RemoteDMATransfer
from concourse.mybir import dt, AluOpType, ActivationFunctionType

F32, BF, I32, U16 = "float32", "bfloat16", "int32", "uint16"
CODE, PLANE = "float8_e4m3fn_x4", "uint8"
SCRATCH = {
    "ut": ("sbuf", [128, 512], BF),
    "xt": ("sbuf", [128, 2048], BF), "wt": ("sbuf", [128, 2048], BF),
    "uq": ("sbuf", [128, 128], CODE), "up": ("sbuf", [128, 128], PLANE),
    "urq": ("sbuf", [128, 128], CODE), "urp": ("sbuf", [128, 128], PLANE),
    "xq": ("sbuf", [128, 512], CODE), "xp": ("sbuf", [128, 512], PLANE),
    "wq": ("sbuf", [128, 512], CODE), "wp": ("sbuf", [128, 512], PLANE),
    "slotq": ("sbuf", [128, 512], CODE), "slotp": ("sbuf", [128, 512], PLANE),
    "landq": ("sbuf", [128, 512], CODE), "landp": ("sbuf", [128, 512], PLANE),
    "finq": ("sbuf", [128, 512], CODE), "finp": ("sbuf", [128, 512], PLANE),
    "zoff": ("sbuf", [128, 8], U16), "colidx": ("sbuf", [128, 256], F32),
    "mk0": ("sbuf", [128, 256], F32), "mk1": ("sbuf", [128, 256], F32),
    "pi": ("sbuf", [128, 1], I32), "pa": ("sbuf", [128, 1], I32), "pb": ("sbuf", [128, 1], I32),
    "pf": ("sbuf", [128, 1], F32), "paf": ("sbuf", [128, 1], F32), "pbf": ("sbuf", [128, 1], F32),
    "tc0": ("sbuf", [128, 1], F32), "tc1": ("sbuf", [128, 1], F32), "g64": ("sbuf", [128, 1], F32),
    "vfree": ("sbuf", [128, 64], F32), "vals": ("sbuf", [128, 64], BF),
    "colf": ("sbuf", [32, 32], F32), "ocol": ("dram", [128, 4], F32), "rcol": ("dram", [8, 128, 4], F32),
    "cr": ("sbuf", [128, 512], F32), "idb": ("sbuf", [128, 512], F32), "yb": ("sbuf", [128, 512], F32),
}
for _k in "ab":
    for _n, _w, _d in (("sa", 64, F32), ("sb", 64, F32), ("dl", 4, F32), ("thr", 1024, F32), ("cmp", 2048, BF),
                       ("rel", 512, BF), ("sgn", 512, BF), ("nlt", 8, F32), ("so", 1024, BF),
                       ("pl", 4, U16), ("sw", 512, BF), ("tr", 512, BF), ("ya", 32, BF), ("yt", 32, BF),
                       ("za", 32, BF), ("zb", 32, BF), ("uu", 64, BF), ("vt", 64, BF), ("off", 32, U16)):
        SCRATCH[_n + _k] = ("sbuf", [128, _w], _d)
for _k in range(8):
    SCRATCH["ps%d" % _k] = ("psum", [128, 512], F32)

SEMAPHORES = ["cv", "cs", "ct", "cg", "du", "dx0", "dx1", "dw", "dc", "dr", "dy", "di",
              "ara", "arb", "arc", "ls"]

PLAN = {"va": "m0 T0 m1 q1 t0 T1 i0 x2 i1 x0 x1 i2 z0 z1 i3 z2 z3", "sa": "d0 t1 d1 t2 r3 t3 s3",
        "vb": "T0 T1 x1 t1 x2 x0 i0 i2 i1 z0 z2 i3 z1 z3", "sb": "d0 d1 t0 t2 r3 t3 s3"}


def rank_program(g, core, T, topo):
    me = T.rank_of(core)
    if me is None:
        return
    V, S, P, Y = g.vector, g.scalar, g.tensor, g.sync
    AF = ActivationFunctionType
    Copy, Ident = AF.Copy, AF.Identity
    GT, GE, LT = AluOpType.is_gt, AluOpType.is_ge, AluOpType.is_lt
    ADD, MUL, AND = AluOpType.add, AluOpType.mult, AluOpType.bitwise_and
    cnt, seen = {}, {}
    queue = {"v": V, "s": S, "t": P, "g": g, "y": Y}
    CORES = T.cores
    N = len(CORES)
    CH = 512 // N

    def need(q, *toks):
        for sem, val in toks:
            if seen.get((q, sem), 0) < val:
                queue[q].wait_ge(T.sem[sem], val)
                seen[(q, sem)] = val

    def done(q, inst):
        sem = "c" + q
        inst.then_inc(T.sem[sem], 1)
        cnt[sem] = cnt.get(sem, 0) + 1
        return (sem, cnt[sem])

    def dma(sem, inst):
        inst.then_inc(T.sem[sem], 16)
        cnt[sem] = cnt.get(sem, 0) + 16
        return (sem, cnt[sem])

    tu = dma("du", S.dma_start(T.ut[:, 0:8], T.u[:, 0:8]))
    tx = [dma("dx0", Y.dma_start(T.xt[:, 0:1024], T.x[:, 0:1024])),
          dma("dx1", S.dma_start(T.xt[:, 1024:2048], T.x[:, 1024:2048]))]
    need("y", *tx)
    dma("dw", Y.dma_start(T.wt[:, 0:1024], T.w[:, 0:1024]))
    tw = dma("dw", Y.dma_start(T.wt[:, 1024:2048], T.w[:, 1024:2048]))

    tpi = done("g", g.iota(T.pi[:], [[1, 1]], 0, 1))
    tpf = done("g", g.iota(T.pf[:], [[1, 1]], 0, 1, allow_small_or_imprecise_dtypes=True))
    tci = done("g", g.iota(T.colidx[:], [[1, 256]], 0, 0, allow_small_or_imprecise_dtypes=True))
    tvf = done("g", g.iota(T.vfree[:], [[256, 2], [32, 2], [1, 16]], -256, 0, allow_small_or_imprecise_dtypes=True))
    tcr = done("g", g.iota(T.cr[:], [[1, N], [0, CH]], 0, 0, allow_small_or_imprecise_dtypes=True))

    done("v", V.memset(T.ut[:, 8:512], 0.0))
    tz = done("v", V.memset(T.zoff[:], 0))
    need("v", tpi)
    done("v", V.tensor_scalar(T.pa[:], T.pi[:], 96, None, AND))
    t = done("v", V.tensor_scalar(T.pb[:], T.pi[:], 16, None, AND))
    done("v", V.memset(T.swa[:], 0.0))
    need("v", t)
    done("v", V.tensor_copy(T.paf[:], T.pa[:]))
    tpb = done("v", V.tensor_copy(T.pbf[:], T.pb[:]))

    need("v", tu, tz)
    tq = done("v", V.quantize_mx(T.uq[:], T.up[:], T.ut[:]))
    need("v", tpf, tpb)
    done("v", V.tensor_tensor(T.tc0[:], T.pf[:], T.paf[:], ADD))
    tg64 = done("v", V.tensor_scalar(T.g64[:], T.paf[:], 2.0, T.pbf[:], MUL, ADD))
    need("v", tq)
    tur = done("v", V.tensor_copy(T.urq[:].bitcast(dt.uint32), T.uq[:].bitcast(dt.uint32).indirect(T.zoff[:])))
    need("s", tq, tz)
    tup = done("s", S.activation(T.urp[:], T.up[:].indirect(T.zoff[:]), Copy))
    need("v", tg64)
    ttc = done("v", V.tensor_scalar(T.tc1[:], T.tc0[:], 32.0, None, ADD))

    MK = (T.mk0, T.mk1)
    mkt = {}

    def mask(i):
        need("v", tci, ttc)
        mkt[i] = done("v", V.tensor_scalar(MK[i][:], T.colidx[:], (T.tc0, T.tc1)[i][:], -1.0, LT, MUL))
        if i == 1:
            need("v", tvf)
            done("v", V.tensor_scalar(T.vals[:], T.vfree[:], T.g64[:], None, ADD))
            done("v", V.memset(T.yaa[:, 16:32], 0.0))
        return mkt[i]

    H = (slice(0, 64), slice(64, 128))
    Q = [slice(32 * a, 32 * a + 32) for a in range(4)]

    def row(ps, q, p, a, b, *toks):
        need("t", tur, tup, *toks)
        return done("t", P.matmul_mx(ps[:, 0:b - a], T.urq[:], T.urp[:], q[:, a:b], p[:, a:b], True, True))

    def own(k, c):
        return T[("sa", "sb")[c // 2] + k][:, 32 * (c % 2):32 * (c % 2) + 1]

    def count(k, R, RS, tok, second=None):
        cm, so, th, dl, rel, sgn, nlt = [T[n + k] for n in ("cmp", "so", "thr", "dl", "rel", "sgn", "nlt")]
        vplan = PLAN["v" + k].split()
        plan = {"v": list(vplan), "s": PLAN["s" + k].split()}
        tok = dict(tok)
        tok.update({"m%d" % i: mkt[i] for i in mkt})
        front = ["i0", "i1"] + [x for x in vplan if x in ("x2", "x3")]

        def deps(w):
            c = int(w[1])
            h = c // 2
            return {"q": [], "m": [], "T": ["R%d" % c], "d": ["T%d" % c], "t": ["d%d" % h, "m%d" % (c % 2)], "i": ["t%d" % c],
                    "x": ["T%d" % h, "R%d" % (1 - h)], "r": ["T%d" % h] + (front if RS is None else ["RS"]),
                    "s": ["r%d" % c], "z": ["i%d" % c, ("x%d" if "x%d" % c in vplan else "s%d") % c]}[w[0]]

        def emit(q, w):
            c = int(w[1])
            h, at, o = c // 2, 512 * c, 256 * (c % 2)
            if w[0] == "q":
                return second()
            if w[0] == "m":
                return mask(c)
            need(q, *[tok[x] for x in deps(w)])
            if w[0] == "T":
                for a in range(4):
                    tk = done("v", V.transpose(T[("sa", "sb")[c] + k][Q[a], 0:64], R[c][Q[a], 64 * a:64 * a + 64]))
                return tk
            if w[0] == "d":
                return done("s", S.activation(dl[:, 2 * c:2 * c + 2], T[("sa", "sb")[c] + k][:, 0:64:32], AF.Abs,
                                              bias=2.0 ** -120, scale=0.6 * 2.0 ** -23))
            if w[0] == "t":
                to = th[:, 256 * c:256 * c + 256]
                if q == "s":
                    return done("s", S.activation(to, MK[c % 2][:], Ident, bias=own(k, c), scale=dl[:, c:c + 1]))
                return done("v", V.tensor_scalar(to, MK[c % 2][:], dl[:, c:c + 1], own(k, c), MUL, ADD))
            if w[0] == "i":
                return done("v", V.tensor_tensor(cm[:, at:at + 256], R[h][:, 0:256], th[:, 256 * c:256 * c + 256], GT))
            if w[0] == "x":
                return done("v", V.tensor_scalar(cm[:, at + 256:at + 512], R[1 - h][:, 0:256], own(k, c), None, (GT, GE)[h]))
            if w[0] == "r":
                src = R[0] if RS is None else RS
                return done("s", S.activation(rel[:, o:o + 256], src[:, 0:256], AF.Relu, bias=own(k, c), scale=-1.0))
            if w[0] == "s":
                return done("s", S.activation(sgn[:, o:o + 256], rel[:, o:o + 256], AF.Sign, scale=-1.0,
                                              accum_out=nlt[:, 4 * (c % 2):4 * (c % 2) + 1]))
            if "x%d" % c in vplan:
                return done("v", V.tensor_tensor_scan(so[:, 256 * c:256 * c + 256], cm[:, at:at + 256], cm[:, at + 256:at + 512],
                                                      -256.0, ADD, ADD))
            return done("v", V.tensor_tensor_scan(so[:, 256 * c + 128:256 * c + 256], cm[:, at:at + 128], cm[:, at + 128:at + 256],
                                                  nlt[:, 4 * (c % 2):4 * (c % 2) + 1], ADD, ADD))

        while plan["v"] or plan["s"]:
            for q in "vs":
                while plan[q] and all(x in tok for x in deps(plan[q][0])):
                    w = plan[q].pop(0)
                    tok["R1" if w == "q1" else w] = emit(q, w)
        return tok[vplan[-1]]

    def make_list(k, tok):
        pl, sw, tr, ya, yt, za, zb, uu, vt, off = [T[n + k] for n in ("pl", "sw", "tr", "ya", "yt", "za", "zb", "uu", "vt", "off")]
        need("v", tok)
        tk = done("v", V.tensor_scalar(pl[:], T["so" + k][:, 255:1024:256], 256.0, None, ADD))
        need("v", tk)
        tk = done("v", V.tensor_copy(sw[:, 0:512].indirect(pl[:]), T.vals[:]))
        need("v", tk)
        tk = done("v", V.transpose(tr[:], sw[:]))
        need("v", tk)
        tk = done("v", V.tensor_tensor(ya[:, 0:16], tr[:, 0:512:32], tr[:, 16:512:32], ADD))
        need("v", tk)
        tk = done("v", V.transpose(yt[:], ya[:]))
        need("v", tk)
        done("v", V.tensor_tensor(za[H[0], :], yt[H[0], :], yt[H[1], :], ADD))
        for a in range(2):
            tk = done("v", V.tensor_tensor(zb[Q[a], :], yt[Q[a ^ 1], :], yt[Q[a ^ 3], :], ADD))
        need("v", tk)
        for j in (1, 2, 0, 3):
            h = 16 * (j // 2)
            tk = done("v", V.tensor_tensor(uu[H[0], 16 * j:16 * j + 16], za[H[0], h:h + 16], zb[H[0], h:h + 16], ADD))
            if j == 2:
                tf = tk
        need("v", tk)
        tk = done("v", V.transpose(vt[H[0], :], uu[H[0], :]))
        need("v", tk)
        for r in H:
            done("v", V.tensor_scalar(off[r, 0:32:2], vt[H[0], 0:16], 256.0, None, ADD))
            tk = done("v", V.tensor_scalar(off[r, 1:32:2], vt[H[0], 32:48], 256.0, None, ADD))
        return tf, tk

    RA, RB = T.ps0, T.ps1

    def quant(h):
        need("v", tx[h])
        a, b = 256 * h, 256 * h + 256
        return done("v", V.quantize_mx(T.xq[:, a:b], T.xp[:, a:b], T.xt[:, 4 * a:4 * b]))

    tra = row(RA, T.xq, T.xp, 0, 256, quant(0))
    tcount = count("a", (RA, RB), None, {"R0": tra}, lambda: row(RB, T.xq, T.xp, 256, 512, quant(1)))
    tfo, tof = make_list("a", tcount)

    need("s", tfo)
    tcf = done("s", S.activation(T.colf[:], T.uua[Q[0], 16:48], Ident, bias=256.0))
    need("v", tof)
    need("s", tof)

    def codes(dst, src, off, a, b):
        return done("v", V.tensor_copy(dst[:, a:b].bitcast(dt.uint32), src[:].bitcast(dt.uint32).indirect(off[:, a // 16:b // 16])))

    def scales(dst, src, off, a, b):
        return done("s", S.activation(dst[:, a:b], src[:].indirect(off[:, a // 16:b // 16]), Copy))

    def firsts(s):
        return (N - 2, N - 1) if s < N // 2 else (0, 1)

    lo, hi = (CH if me == 0 else 0), (512 - CH if me == N - 1 else 512)
    fa, fb = CH * firsts(me)[0], CH * firsts(me)[1] + CH
    rest = (lo, fa) if fa else (fb, hi)
    tsc1 = scales(T.slotp, T.xp, T.offa, fa, fb)
    tsc2 = scales(T.slotp, T.xp, T.offa, *rest)
    codes(T.slotq, T.xq, T.offa, fa, fb)
    tcode = codes(T.slotq, T.xq, T.offa, *rest)
    ov = codes(T.landq, T.xq, T.offa, CH * me, CH * me + CH)
    osc = scales(T.landp, T.xp, T.offa, CH * me, CH * me + CH)

    others = [d for d in range(N) if d != me]
    far = [d for d in others if topo.die(CORES[d]) != topo.die(core)]
    near = [d for d in others if d not in far]
    masks, wide = {}, {}
    for grp, first in ((far, 0), (near, 1)):
        for i, d in enumerate(grp):
            el = topo.engines(core, CORES[d])
            masks[d] = (1 << el[(4 * i + first) % len(el)]) | (1 << el[(4 * i + first + 2) % len(el)])
    for i, d in enumerate(firsts(me)):
        wide[d] = sum(1 << e for e in topo.engines(core, CORES[d])[i::2])
    NW = len(topo.engines(core, CORES[firsts(me)[0]])) // 2
    order = [others[(i + me) % len(others)] for i in range(len(others))]

    def send(ds, eng, src, dst, sem):
        tl = []
        for d in ds:
            rid, pid, _s = topo.addr(CORES[d])
            tl.append(RemoteDMATransfer(dst_ids=[DstId(rid=rid, pnc=pid)], dma_engine_mask=eng[d],
                                        remote_sem=T.sem[sem], src=src(d), dst=dst))
        g.remote_dma_fused(tl, local_sem=T.sem.ls)
        cnt["ls"] = cnt.get("ls", 0) + len(ds) * (NW if eng is wide else 2)

    here = slice(CH * me, CH * me + CH)
    half = "ara" if me < N // 2 else "arb"
    need("g", tsc1)
    send(firsts(me), wide, lambda d: T.slotp[:, CH * d:CH * d + CH], T.landp[:, here], half)
    need("g", tcode)
    send(order, masks, lambda d: T.slotq[:, CH * d:CH * d + CH].bitcast(dt.uint8), T.landq[:, here].bitcast(dt.uint8), half)
    need("g", tsc2)
    send([d for d in order if d not in firsts(me)], masks, lambda d: T.slotp[:, CH * d:CH * d + CH], T.landp[:, here], half)
    need("y", tcf)
    dma("dc", Y.dma_start(T.ocol[:], T.colf[0:16, :]))
    tdc = dma("dc", Y.dma_start(T.rcol[me], T.colf[0:16, :]))
    need("g", tdc)
    send(order, masks, lambda d: T.ocol[:], T.rcol[me], "arc")
    need("y", tdc, ("arc", 2 * (N - 1)), tcr)
    tdr = dma("dr", Y.dma_start(T.cr[1:2, :], T.rcol[:, CH // 4 * me:CH // 4 * me + CH // 4, :]))

    done("v", V.memset(T.swb[:], 0.0))
    done("v", V.memset(T.yab[:, 16:32], 0.0))
    need("v", tw)
    twq = done("v", V.quantize_mx(T.wq[:], T.wp[:], T.wt[:]))

    def landed(ranks):
        return sum(2 + (NW if me in firsts(s) else 2) for s in ranks if s != me)

    SA, SB, SC = T.ps3, T.ps4, T.ps5
    tsa = row(SA, T.landq, T.landp, 0, 256, ("ara", landed(range(N // 2))), *((ov, osc) if me < N // 2 else ()))
    tsb = row(SB, T.landq, T.landp, 256, 512, ("arb", landed(range(N // 2, N))), ov, osc)
    tsc = row(SC, T.landq, T.landp, 0, 256)
    _f, tof = make_list("b", count("b", (SA, SB), SC, {"R0": tsa, "R1": tsb, "RS": tsc}))

    need("v", tof)
    need("s", tof)
    YP = (T.ps6, T.ps7, T.ps0, T.ps1)
    ty = []
    for k in range(4):
        a, b = 128 * k, 128 * k + 128
        if k % 2 == 0:
            tv = codes(T.finq, T.landq, T.offb, a, a + 256)
            ts = scales(T.finp, T.landp, T.offb, a, a + 256)
        need("t", twq, tv, ts)
        ty.append(done("t", P.matmul_mx(YP[k][:, 0:128], T.wq[:, a:b], T.wp[:, a:b], T.finq[:, a:b], T.finp[:, a:b], True, True)))
    for k in (0, 2):
        for b in (k, k + 1):
            need("v", ty[b])
            t = done("v", V.tensor_copy(T.yb[:, 128 * b:128 * b + 128], YP[b][:, 0:128]))
        need("y", t)
        dma("dy", Y.dma_start(T.y[:, 128 * k:128 * k + 256], T.yb[:, 128 * k:128 * k + 256]))
    need("v", tdr)
    ti1 = done("v", V.tensor_copy(T.idb[:, 0:128], T.cr[:].indirect(T.offb[:, 0:8])))
    need("s", tdr)
    ti2 = done("s", S.activation(T.idb[:, 128:512], T.cr[:].indirect(T.offb[:, 8:32]), Copy))
    need("s", ti1, ti2)
    dma("di", S.dma_start(T.ids[:], T.idb[0:2, :]))

    for sem in ("cv", "cs", "ct", "cg", "dw", "dy", "di", "ls"):
        need("g", (sem, cnt[sem]))
